import numpy as np, ml_dtypes
CORES = [2,3,42,43,82,83,122,123]
N = 8
import mx_ref
BF = ml_dtypes.bfloat16
def gentries(a):
    return np.ascontiguousarray(a.reshape(8, 16, -1).transpose(0, 2, 1)).reshape(8, -1)
def gtable(e):
    e = np.asarray(e); return np.ascontiguousarray(e.reshape(8, -1, 16).transpose(0, 2, 1)).reshape(128, -1).astype(np.int32)
def gcols(t, e):
    v = np.concatenate([t.reshape(8, 16, -1, 4), np.zeros((8, 16, 1, 4), BF)], axis=2)
    return np.ascontiguousarray(np.stack([v[g][:, e[g]] for g in range(8)])).reshape(128, -1)
def f(rng, *shape):
    return mx_ref.flush((rng.standard_normal(shape, dtype=np.float32) * np.exp2(rng.integers(-2, 3, shape[:-1] + (1,)))).astype(BF))
def wide(rng, *shape, cols=0):
    v = rng.standard_normal(shape, dtype=np.float32) * np.exp2(rng.integers(-12, 13, shape)).astype(np.float32)
    if cols: v *= np.repeat(np.exp2(rng.integers(-cols, cols + 1, shape[:-2] + (1, shape[-1] // 4))) * (rng.random(shape[:-2] + (1, shape[-1] // 4)) > 0.0625), 4, axis=-1).astype(np.float32)
    return mx_ref.flush(v.astype(BF))
S = 256
def block(rng, how):
    if how == "one": return np.full((8, S), rng.integers(0, 128))
    if how == "groups": return np.tile(rng.integers(0, 128, S), (8, 1))
    if how == "ends": return np.stack([rng.permutation(np.arange(S) % 2 * 127) for g in range(8)])
    if how == "distinct": return np.stack([np.tile(rng.permutation(128), S // 128) for g in range(8)])
    return rng.integers(0, 128, (8, S))
def lists(rng, how=""):
    return {"cw": np.stack([gtable(np.concatenate([block(rng, how) for s in range(N)], axis=1)) for r in range(N)])}
def setup_inputs(rng):
    return {"bk": f(rng, N, 128, 512), "x": f(rng, N, 128, 512 * N), **lists(rng)}
def setup_inputs_one(rng):
    return {**setup_inputs(rng), **lists(rng, "one")}
def setup_inputs_groups(rng):
    return {**setup_inputs(rng), **lists(rng, "groups")}
def setup_inputs_ends(rng):
    return {**setup_inputs(rng), **lists(rng, "ends")}
def setup_inputs_distinct(rng):
    return {**setup_inputs(rng), **lists(rng, "distinct")}
def setup_inputs_spread(rng):
    d = setup_inputs(rng); d["bk"] = wide(rng, N, 128, 512, cols=4); d["x"] = wide(rng, N, 128, 512 * N); return d
def check_inputs(d):
    b = []
    for r in range(N):
        e = d["cw"][r]
        if e.min() < 0 or e.max() > 127: b.append("cw")
    return b
def reference(bk, x, cw):
    y = np.zeros((N, 128, S), np.float32)
    for r in range(N):
        e = gentries(cw[r])
        for s in range(N):
            W = gcols(bk[s], e[:, S * s:S * s + S])
            X = np.ascontiguousarray(x[r][:, 512 * s:512 * s + 512])
            y[r] += mx_ref.matmul(mx_ref.quantize(X), mx_ref.quantize(W))
    return {"y": y}

@@ -1,0 +1,239 @@
+from concourse.mybir import dt, AluOpType, ActivationFunctionType
+from concourse.bass import DstId, RemoteDMATransfer
+
+N = 8
+S = 256
+L = S // 16
+ORDER = (3, 2, 5, 7, 6, 4, 1)
+VIA = (True, False, True, True, False, False, False)
+STEPS = ((0,), (1, 2), (3,), (4,), (5,), (6,))
+SHARE = ((2, 3), (2, 3, 1), (1, 2, 3), (2, 3), (1, 2, 3), (2, 3))
+LISTS = ((0, 1), (2, 3), (4, 5, 6))
+ARRIVAL = (1, 0, 2, 4, 3, 6, 5)
+
+SCRATCH = {
+    "cwi": ("sbuf", [128, N * L], "int32"),
+    "cwu": ("sbuf", [128, N * L], "uint16"),
+    "lst": ("sbuf", [128, 7 * L], "uint16"),
+    "bks": ("sbuf", [128, 512], "bfloat16"),
+    "bkp": ("sbuf", [128, 512], "bfloat16"),
+    "xs": ("sbuf", [128, 512 * N], "bfloat16"),
+    "xq": ("sbuf", [128, 128 * N], "float8_e4m3fn_x4"),
+    "xz": ("sbuf", [128, 128 * N], "uint8"),
+    "w": ("sbuf", [128, 4 * S * N], "bfloat16"),
+    "wq": ("sbuf", [128, S * N], "float8_e4m3fn_x4"),
+    "wz": ("sbuf", [128, S * N], "uint8"),
+    "rq": ("sbuf", [128, S * 7], "float8_e4m3fn_x4"),
+    "rz": ("sbuf", [128, S * 7], "uint8"),
+    "yp": ("psum", [128, 512], "float32"),
+    "ys": ("sbuf", [128, S], "float32"),
+}
+SEMAPHORES = (["ldc", "ldb", "ldx0", "ldx1", "conv", "plv", "pls", "lsent", "wsent", "fsent", "qself", "gvs", "gss",
+               "xq0", "xq1", "mm", "cp", "st"]
+              + ["l%d" % k for k in range(7)] + ["a%d" % k for k in range(7)]
+              + ["rc%d" % k for k in range(7)] + ["rz%d" % k for k in range(7)]
+              + ["gv%d" % i for i in range(6)] + ["gs%d" % i for i in range(6)] + ["q%d" % i for i in range(6)])
+
+
+def bits(engines):
+    return sum(1 << e for e in engines)
+
+
+def dest(core, topo):
+    rid, pid, _ = topo.addr(core)
+    return DstId(rid=rid, pnc=pid)
+
+
+def relay_of(rank, slot, T, topo):
+    if not VIA[slot]:
+        return None
+    src, dst = T.cores[rank], T.cores[rank ^ ORDER[slot]]
+    cand = [c for c in topo.cores_of(src)
+            if T.rank_of(c) is None and topo.may_write(c, dst) and topo.die(c) != topo.die(src)]
+    reach = {c: sum(topo.may_write(c, d) for d in T.cores) for c in cand}
+    cand = [c for c in cand if reach[c] == min(reach.values())]
+    mine = [c for c in T.cores if topo.chip(c) == topo.chip(src)]
+    return cand[mine.index(src) % len(cand)]
+
+
+def off_chip(rank, T, topo):
+    return topo.engines(T.cores[rank], T.cores[rank ^ ORDER[0]])
+
+
+def first_engines(rank, slot, T, topo):
+    src, dst = T.cores[rank], T.cores[rank ^ ORDER[slot]]
+    off = off_chip(rank, T, topo)
+    via = relay_of(rank, slot, T, topo)
+    to = dst if via is None else via
+    if topo.chip(src) != topo.chip(to):
+        return off
+    engines = topo.engines(src, to)
+    return engines if slot == 0 else [e for e in engines if e not in off]
+
+
+def forward(g, core, T, topo):
+    total = 0
+    for slot in range(7):
+        for rank in range(N):
+            if relay_of(rank, slot, T, topo) != core:
+                continue
+            dst = T.cores[rank ^ ORDER[slot]]
+            rid, pid, _ = topo.addr(dst)
+            mask = topo.mask(core, dst)
+            came = len(first_engines(rank, slot, T, topo))
+            c = slice(slot * S, slot * S + S)
+            view = T.rq[:, c].bitcast(dt.uint8)
+            g.wait_ge(T.sem["rc%d" % slot], came)
+            g.remote_dma(out_ap=view, in_ap=view, remote_sem=T.sem["a%d" % slot], local_sem=T.sem.fsent,
+                         pid=pid, routing_id=rid, dma_engine_mask=mask)
+            g.wait_ge(T.sem["rz%d" % slot], came)
+            g.remote_dma(out_ap=T.rz[:, c], in_ap=T.rz[:, c], remote_sem=T.sem["a%d" % slot], local_sem=T.sem.fsent,
+                         pid=pid, routing_id=rid, dma_engine_mask=mask)
+            total += 2 * len(topo.engines(core, dst))
+    if total:
+        g.wait_ge(T.sem.fsent, total)
+
+
+def rank_program(g, core, T, topo):
+    rank = T.rank_of(core)
+    if rank is None:
+        forward(g, core, T, topo)
+        return
+    sem = T.sem
+    off = off_chip(rank, T, topo)
+    half = len(off) // 2
+    rest = [e for e in topo.engines(core, T.cores[rank ^ ORDER[6]]) if e not in off]
+    COPY = ActivationFunctionType.Copy
+
+    g.sync.dma_start(T.cwi[:], T.cw[:]).then_inc(sem.ldc, 16)
+    h = 512 * N // 2
+    g.sync.dma_start(T.xs[:, 0:h], T.x[:, 0:h]).then_inc(sem.ldx0, 16)
+
+    g.wait_ge(sem.conv, 1)
+    lsent = 0
+    for call in LISTS:
+        tr = []
+        for slot, eng in zip(call, (off[:half], off[half:], rest)):
+            p = rank ^ ORDER[slot]
+            tr.append(RemoteDMATransfer(dst_ids=[dest(T.cores[p], topo)], dma_engine_mask=bits(eng),
+                                        remote_sem=sem["l%d" % slot], src=T.cwu[:, p * L:p * L + L],
+                                        dst=T.lst[:, slot * L:slot * L + L]))
+            lsent += len(eng)
+        g.remote_dma_fused(tr, local_sem=sem.lsent)
+    g.sync.wait_ge(sem.lsent, lsent)
+    g.sync.dma_start(T.xs[:, h:2 * h], T.x[:, h:2 * h]).then_inc(sem.ldx1, 16)
+
+    def listed(queue, slot):
+        queue.wait_ge(sem["l%d" % slot], half if slot < 6 else len(rest))
+
+    wsent = 0
+    for i, step in enumerate(STEPS):
+        g.wait_ge(sem["q%d" % i], 1)
+        for what in range(2):
+            tr = []
+            for slot in step:
+                via = relay_of(rank, slot, T, topo)
+                a = (slot + 1) * S
+                if what == 0:
+                    src, out = T.wq[:, a:a + S].bitcast(dt.uint8), T.rq[:, slot * S:slot * S + S].bitcast(dt.uint8)
+                else:
+                    src, out = T.wz[:, a:a + S], T.rz[:, slot * S:slot * S + S]
+                if via is None:
+                    to, s = T.cores[rank ^ ORDER[slot]], sem["a%d" % slot]
+                else:
+                    to, s = via, sem[("rc%d" if what == 0 else "rz%d") % slot]
+                eng = first_engines(rank, slot, T, topo)
+                tr.append(RemoteDMATransfer(dst_ids=[dest(to, topo)], dma_engine_mask=bits(eng), remote_sem=s,
+                                            src=src, dst=out))
+                wsent += len(eng)
+            g.remote_dma_fused(tr, local_sem=sem.wsent)
+    g.wait_ge(sem.wsent, wsent)
+
+    g.scalar.dma_start(T.bks[:], T.bk[:]).then_inc(sem.ldb, 16)
+    g.scalar.wait_ge(sem.ldb, 16)
+    for t in (2, 3):
+        g.scalar.activation(T.bkp[:, t * 128:t * 128 + 128], T.bks[:, t:512:4], COPY).then_inc(sem.pls, 1)
+
+    def window(t):
+        return T.bkp[:, t * 128:t * 128 + 128]
+
+    def place(t, slot, n):
+        a = (slot + 1) * 4 * S
+        return T.w[:, a + t:a + n * 4 * S:4]
+
+    def gathers(i, scalar):
+        step, mine = STEPS[i], SHARE[i]
+        if len(step) == 1:
+            return [(t, step[0], 1) for t in range(4) if (t in mine) == scalar]
+        if scalar:
+            return [(2, step[0], 2), (3, step[0], 2), (1, step[1], 1)]
+        return [(0, step[0], 2), (1, step[0], 1)]
+
+    mylist = T.cwu[:, rank * L:rank * L + L]
+    g.scalar.wait_ge(sem.pls, 2)
+    g.scalar.wait_ge(sem.conv, 1)
+    for t in (2, 3):
+        g.scalar.activation(place(t, -1, 1), window(t).indirect(mylist), COPY).then_inc(sem.gss, 1)
+    g.scalar.wait_ge(sem.plv, 2)
+    for i, step in enumerate(STEPS):
+        for slot in step:
+            listed(g.scalar, slot)
+        for t, a, n in gathers(i, True):
+            g.scalar.activation(place(t, a, n), window(t).indirect(T.lst[:, a * L:(a + n) * L]), COPY).then_inc(sem["gs%d" % i], 1)
+
+    g.vector.wait_ge(sem.ldc, 16)
+    g.vector.tensor_copy(T.cwu[:], T.cwi[:]).then_inc(sem.conv, 1)
+    g.vector.wait_ge(sem.ldb, 16)
+    for t in (0, 1):
+        g.vector.tensor_copy(T.bkp[:, t * 128:t * 128 + 128], T.bks[:, t:512:4]).then_inc(sem.plv, 1)
+    g.vector.wait_ge(sem.plv, 2)
+    g.vector.wait_ge(sem.conv, 1)
+    for t in (0, 1):
+        g.vector.tensor_copy(place(t, -1, 1), window(t).indirect(mylist)).then_inc(sem.gvs, 1)
+    g.vector.wait_ge(sem.gvs, 2)
+    g.vector.wait_ge(sem.gss, 2)
+    g.vector.quantize_mx(T.wq[:, 0:S], T.wz[:, 0:S], T.w[:, 0:4 * S]).then_inc(sem.qself, 1)
+
+    def quantise_x(b):
+        g.vector.wait_ge(sem["ldx%d" % b], 16)
+        c = slice(b * 512, b * 512 + 512)
+        g.vector.quantize_mx(T.xq[:, c], T.xz[:, c], T.xs[:, b * 2048:b * 2048 + 2048]).then_inc(sem["xq%d" % b], 1)
+
+    quantise_x(0)
+    for i, step in enumerate(STEPS):
+        if i == len(STEPS) - 1:
+            quantise_x(1)
+        for slot in step:
+            listed(g.vector, slot)
+        for t, a, n in gathers(i, False):
+            g.vector.tensor_copy(place(t, a, n), window(t).indirect(T.lst[:, a * L:(a + n) * L])).then_inc(sem["gv%d" % i], 1)
+        g.vector.wait_ge(sem["gv%d" % i], len(gathers(i, False)))
+        g.vector.wait_ge(sem["gs%d" % i], len(gathers(i, True)))
+        a, n = step[0], len(step)
+        c = slice((a + 1) * S, (a + 1 + n) * S)
+        g.vector.quantize_mx(T.wq[:, c], T.wz[:, c],
+                             T.w[:, (a + 1) * 4 * S:(a + 1 + n) * 4 * S]).then_inc(sem["q%d" % i], 1)
+
+    def product(s, codes, scales, start, stop):
+        c = slice(s * 128, s * 128 + 128)
+        r = g.tensor.matmul_mx(T.yp[:, 0:S], T.xq[:, c], T.xz[:, c], codes, scales, start, stop)
+        if stop:
+            r.then_inc(sem.mm, 1)
+
+    g.tensor.wait_ge(sem.xq0, 1)
+    g.tensor.wait_ge(sem.xq1, 1)
+    g.tensor.wait_ge(sem.qself, 1)
+    product(rank, T.wq[:, 0:S], T.wz[:, 0:S], True, False)
+    for j, slot in enumerate(ARRIVAL):
+        p = rank ^ ORDER[slot]
+        via = relay_of(p, slot, T, topo)
+        count = len(first_engines(p, slot, T, topo) if via is None else topo.engines(via, core))
+        g.tensor.wait_ge(sem["a%d" % slot], 2 * count)
+        c = slice(slot * S, slot * S + S)
+        product(p, T.rq[:, c], T.rz[:, c], False, j == 6)
+
+    g.vector.wait_ge(sem.mm, 1)
+    g.vector.tensor_copy(T.ys[:], T.yp[:, 0:S]).then_inc(sem.cp, 1)
+    g.sync.wait_ge(sem.cp, 1)
+    g.sync.dma_start(T.y[:], T.ys[:]).then_inc(sem.st, 16)
+    g.sync.wait_ge(sem.st, 16)

@@ -1,15 +1,23 @@
-from concourse.mybir import dt, AluOpType, ActivationFunctionType
+from concourse.mybir import dt, ActivationFunctionType
 from concourse.bass import DstId, RemoteDMATransfer
 
 N = 8
 S = 256
 L = S // 16
-ORDER = (3, 2, 5, 7, 6, 4, 1)
-VIA = (True, False, True, True, False, False, False)
-STEPS = ((0,), (1, 2), (3,), (4,), (5,), (6,))
-SHARE = ((2, 3), (2, 3, 1), (1, 2, 3), (2, 3), (1, 2, 3), (2, 3))
-LISTS = ((0, 1), (2, 3), (4, 5, 6))
-ARRIVAL = (1, 0, 2, 4, 3, 6, 5)
+H = S // 2
+CORES_IN_ALL = 128
+ORDER = (3, 5, 2, 7, 6, 4, 1)
+DIRECT = ("qz", ((), "off"))
+WAYS = ((("zq", (("near", "mate near"), "all")), ("zq", (("far", "mate far"), "all"))),
+        (("zq", (("wide",), "all")), DIRECT),
+        (DIRECT, ("zq", (("wide",), "rest"))),
+        (("qz", (("wide",), "rest")), DIRECT),
+        (DIRECT, ("qz", (("wide",), "rest"))),
+        (DIRECT, DIRECT),
+        (("qz", ((), "rest")),) * 2)
+VPLANES = (2, 2, 1, 2, 2, 1, 1)
+LISTS = ((0,), (1, 2), (3, 4), (5, 6))
+ARRIVAL = (1, 2, 3, 0, 6, 4, 5)
 
 SCRATCH = {
     "cwi": ("sbuf", [128, N * L], "int32"),
@@ -25,14 +33,12 @@ SCRATCH = {
     "wz": ("sbuf", [128, S * N], "uint8"),
     "rq": ("sbuf", [128, S * 7], "float8_e4m3fn_x4"),
     "rz": ("sbuf", [128, S * 7], "uint8"),
-    "yp": ("psum", [128, 512], "float32"),
+    "yp": ("psum", [128, 1024], "float32"),
     "ys": ("sbuf", [128, S], "float32"),
 }
 SEMAPHORES = (["ldc", "ldb", "ldx0", "ldx1", "conv", "plv", "pls", "lsent", "wsent", "fsent", "qself", "gvs", "gss",
-               "xq0", "xq1", "mm", "cp", "st"]
-              + ["l%d" % k for k in range(7)] + ["a%d" % k for k in range(7)]
-              + ["rc%d" % k for k in range(7)] + ["rz%d" % k for k in range(7)]
-              + ["gv%d" % i for i in range(6)] + ["gs%d" % i for i in range(6)] + ["q%d" % i for i in range(6)])
+               "xq0", "xq1", "mm0", "mm1", "cp", "st"]
+              + [n % k for k in range(7) for n in ("l%d", "a%d", "gv%d", "gs%d", "q%d", "rq%d", "rz%d")])
 
 
 def bits(engines):
@@ -44,54 +50,90 @@ def dest(core, topo):
     return DstId(rid=rid, pnc=pid)
 
 
-def relay_of(rank, slot, T, topo):
-    if not VIA[slot]:
-        return None
+def parts(rank, slot):
+    return WAYS[slot][rank % 2][0]
+
+
+def legs_of(rank, slot):
+    return WAYS[slot][rank % 2][1:]
+
+
+def path(rank, slot, leg, T, topo):
     src, dst = T.cores[rank], T.cores[rank ^ ORDER[slot]]
-    cand = [c for c in topo.cores_of(src)
-            if T.rank_of(c) is None and topo.may_write(c, dst) and topo.die(c) != topo.die(src)]
-    reach = {c: sum(topo.may_write(c, d) for d in T.cores) for c in cand}
-    cand = [c for c in cand if reach[c] == min(reach.values())]
-    mine = [c for c in T.cores if topo.chip(c) == topo.chip(src)]
-    return cand[mine.index(src) % len(cand)]
+    way = [dst]
+    for kind in reversed(legs_of(rank, slot)[leg][0]):
+        if kind.startswith("mate"):
+            cand = [c for c in range(CORES_IN_ALL) if topo.mates(topo.chip(c), topo.chip(dst))]
+        else:
+            cand = topo.cores_of(src)
+        cand = [c for c in cand if (topo.die(c) == topo.die(src)) == kind.endswith("near")]
+        cand = [c for c in cand if T.rank_of(c) is None and topo.may_write(c, way[0])]
+        reach = {c: sum(topo.may_write(c, d) for d in T.cores) for c in cand}
+        cand = [c for c in cand if reach[c] == (max if kind == "wide" else min)(reach.values())]
+        mine = [c for c in T.cores if topo.chip(c) == topo.chip(src)]
+        way.insert(0, cand[mine.index(src) % len(cand)])
+    return [src] + way
 
 
-def off_chip(rank, T, topo):
-    return topo.engines(T.cores[rank], T.cores[rank ^ ORDER[0]])
+def engine_sets(rank, T, topo):
+    src = T.cores[rank]
+    every = max((topo.engines(src, c) for c in T.cores if c != src), key=len)
+    off = min((topo.engines(src, c) for c in T.cores if c != src), key=len)
+    rest = [e for e in every if e not in off]
+    return {"all": every, "off": off, "rest": rest, "rest0": rest[0::2], "rest1": rest[1::2]}
 
 
-def first_engines(rank, slot, T, topo):
-    src, dst = T.cores[rank], T.cores[rank ^ ORDER[slot]]
-    off = off_chip(rank, T, topo)
-    via = relay_of(rank, slot, T, topo)
-    to = dst if via is None else via
-    if topo.chip(src) != topo.chip(to):
-        return off
-    engines = topo.engines(src, to)
-    return engines if slot == 0 else [e for e in engines if e not in off]
+def hop_engines(rank, slot, leg, hop, T, topo):
+    if hop == 0:
+        return engine_sets(rank, T, topo)[legs_of(rank, slot)[leg][1]]
+    way = path(rank, slot, leg, T, topo)
+    return topo.engines(way[hop], way[hop + 1])
+
+
+def piece(codes, scales, base, rank, slot, leg, what):
+    n = S // len(legs_of(rank, slot))
+    c = slice(base + leg * n, base + leg * n + n)
+    return codes[:, c].bitcast(dt.uint8) if what == "q" else scales[:, c]
+
+
+def transfer(rank, slot, leg, hop, what, src, T, topo):
+    way = path(rank, slot, leg, T, topo)
+    s = T.sem["a%d" % slot] if hop + 2 == len(way) else T.sem["r%s%d" % (what, slot)]
+    return RemoteDMATransfer(dst_ids=[dest(way[hop + 1], topo)], remote_sem=s, src=src,
+                             dma_engine_mask=bits(hop_engines(rank, slot, leg, hop, T, topo)),
+                             dst=piece(T.rq, T.rz, slot * S, rank, slot, leg, what))
 
 
 def forward(g, core, T, topo):
     total = 0
     for slot in range(7):
         for rank in range(N):
-            if relay_of(rank, slot, T, topo) != core:
-                continue
-            dst = T.cores[rank ^ ORDER[slot]]
-            rid, pid, _ = topo.addr(dst)
-            mask = topo.mask(core, dst)
-            came = len(first_engines(rank, slot, T, topo))
-            c = slice(slot * S, slot * S + S)
-            view = T.rq[:, c].bitcast(dt.uint8)
-            g.wait_ge(T.sem["rc%d" % slot], came)
-            g.remote_dma(out_ap=view, in_ap=view, remote_sem=T.sem["a%d" % slot], local_sem=T.sem.fsent,
-                         pid=pid, routing_id=rid, dma_engine_mask=mask)
-            g.wait_ge(T.sem["rz%d" % slot], came)
-            g.remote_dma(out_ap=T.rz[:, c], in_ap=T.rz[:, c], remote_sem=T.sem["a%d" % slot], local_sem=T.sem.fsent,
-                         pid=pid, routing_id=rid, dma_engine_mask=mask)
-            total += 2 * len(topo.engines(core, dst))
+            for leg in range(len(legs_of(rank, slot))):
+                way = path(rank, slot, leg, T, topo)
+                if core not in way:
+                    continue
+                hop = way.index(core)
+                for what in parts(rank, slot):
+                    g.wait_ge(T.sem["r%s%d" % (what, slot)], len(hop_engines(rank, slot, leg, hop - 1, T, topo)))
+                    src = piece(T.rq, T.rz, slot * S, rank, slot, leg, what)
+                    g.remote_dma_fused([transfer(rank, slot, leg, hop, what, src, T, topo)], local_sem=T.sem.fsent)
+                    total += len(hop_engines(rank, slot, leg, hop, T, topo))
     if total:
         g.wait_ge(T.sem.fsent, total)
+
+
+def list_engines(rank, T, topo):
+    sets, out = engine_sets(rank, T, topo), {}
+    chip = topo.chip(T.cores[rank])
+    for call in LISTS:
+        away = [k for k in call if topo.chip(T.cores[rank ^ ORDER[k]]) != chip]
+        for k in call:
+            if k in away:
+                n, i = len(sets["off"]) // len(away), away.index(k)
+                out[k] = sets["off"][i * n:i * n + n]
+            else:
+                out[k] = sets["rest"]
+    return out
 
 
 def rank_program(g, core, T, topo):
@@ -100,86 +142,66 @@ def rank_program(g, core, T, topo):
         forward(g, core, T, topo)
         return
     sem = T.sem
-    off = off_chip(rank, T, topo)
-    half = len(off) // 2
-    rest = [e for e in topo.engines(core, T.cores[rank ^ ORDER[6]]) if e not in off]
     COPY = ActivationFunctionType.Copy
+    half = [rank // 4, 1 - rank // 4]
+
+    def load_x(b):
+        c = slice(half[b] * 2048, half[b] * 2048 + 2048)
+        g.sync.dma_start(T.xs[:, c], T.x[:, c]).then_inc(sem["ldx%d" % b], 16)
 
     g.sync.dma_start(T.cwi[:], T.cw[:]).then_inc(sem.ldc, 16)
-    h = 512 * N // 2
-    g.sync.dma_start(T.xs[:, 0:h], T.x[:, 0:h]).then_inc(sem.ldx0, 16)
+    g.sync.dma_start(T.bks[:], T.bk[:]).then_inc(sem.ldb, 16)
+    load_x(0)
 
     g.wait_ge(sem.conv, 1)
-    lsent = 0
+    leng = list_engines(rank, T, topo)
     for call in LISTS:
         tr = []
-        for slot, eng in zip(call, (off[:half], off[half:], rest)):
+        for slot in call:
             p = rank ^ ORDER[slot]
-            tr.append(RemoteDMATransfer(dst_ids=[dest(T.cores[p], topo)], dma_engine_mask=bits(eng),
+            tr.append(RemoteDMATransfer(dst_ids=[dest(T.cores[p], topo)], dma_engine_mask=bits(leng[slot]),
                                         remote_sem=sem["l%d" % slot], src=T.cwu[:, p * L:p * L + L],
                                         dst=T.lst[:, slot * L:slot * L + L]))
-            lsent += len(eng)
         g.remote_dma_fused(tr, local_sem=sem.lsent)
-    g.sync.wait_ge(sem.lsent, lsent)
-    g.sync.dma_start(T.xs[:, h:2 * h], T.x[:, h:2 * h]).then_inc(sem.ldx1, 16)
+    g.sync.wait_ge(sem.lsent, sum(len(e) for e in leng.values()))
+    load_x(1)
 
     def listed(queue, slot):
-        queue.wait_ge(sem["l%d" % slot], half if slot < 6 else len(rest))
+        queue.wait_ge(sem["l%d" % slot], len(list_engines(rank ^ ORDER[slot], T, topo)[slot]))
 
     wsent = 0
-    for i, step in enumerate(STEPS):
-        g.wait_ge(sem["q%d" % i], 1)
-        for what in range(2):
-            tr = []
-            for slot in step:
-                via = relay_of(rank, slot, T, topo)
-                a = (slot + 1) * S
-                if what == 0:
-                    src, out = T.wq[:, a:a + S].bitcast(dt.uint8), T.rq[:, slot * S:slot * S + S].bitcast(dt.uint8)
-                else:
-                    src, out = T.wz[:, a:a + S], T.rz[:, slot * S:slot * S + S]
-                if via is None:
-                    to, s = T.cores[rank ^ ORDER[slot]], sem["a%d" % slot]
-                else:
-                    to, s = via, sem[("rc%d" if what == 0 else "rz%d") % slot]
-                eng = first_engines(rank, slot, T, topo)
-                tr.append(RemoteDMATransfer(dst_ids=[dest(to, topo)], dma_engine_mask=bits(eng), remote_sem=s,
-                                            src=src, dst=out))
-                wsent += len(eng)
-            g.remote_dma_fused(tr, local_sem=sem.wsent)
+    for slot in range(7):
+        g.wait_ge(sem["q%d" % slot], 1)
+        legs = range(len(legs_of(rank, slot)))
+        for what in parts(rank, slot):
+            g.remote_dma_fused([transfer(rank, slot, leg, 0, what, piece(T.wq, T.wz, (slot + 1) * S, rank, slot, leg, what), T, topo)
+                                for leg in legs], local_sem=sem.wsent)
+            wsent += sum(len(hop_engines(rank, slot, leg, 0, T, topo)) for leg in legs)
     g.wait_ge(sem.wsent, wsent)
-
-    g.scalar.dma_start(T.bks[:], T.bk[:]).then_inc(sem.ldb, 16)
-    g.scalar.wait_ge(sem.ldb, 16)
-    for t in (2, 3):
-        g.scalar.activation(T.bkp[:, t * 128:t * 128 + 128], T.bks[:, t:512:4], COPY).then_inc(sem.pls, 1)
 
     def window(t):
         return T.bkp[:, t * 128:t * 128 + 128]
 
-    def place(t, slot, n):
+    def place(t, slot):
         a = (slot + 1) * 4 * S
-        return T.w[:, a + t:a + n * 4 * S:4]
+        return T.w[:, a + t:a + 4 * S:4]
 
-    def gathers(i, scalar):
-        step, mine = STEPS[i], SHARE[i]
-        if len(step) == 1:
-            return [(t, step[0], 1) for t in range(4) if (t in mine) == scalar]
-        if scalar:
-            return [(2, step[0], 2), (3, step[0], 2), (1, step[1], 1)]
-        return [(0, step[0], 2), (1, step[0], 1)]
+    def offsets(slot):
+        return T.lst[:, slot * L:slot * L + L]
 
+    g.scalar.wait_ge(sem.ldb, 16)
+    for t in (2, 3):
+        g.scalar.activation(T.bkp[:, t * 128:t * 128 + 128], T.bks[:, t:512:4], COPY).then_inc(sem.pls, 1)
     mylist = T.cwu[:, rank * L:rank * L + L]
     g.scalar.wait_ge(sem.pls, 2)
     g.scalar.wait_ge(sem.conv, 1)
     for t in (2, 3):
-        g.scalar.activation(place(t, -1, 1), window(t).indirect(mylist), COPY).then_inc(sem.gss, 1)
+        g.scalar.activation(place(t, -1), window(t).indirect(mylist), COPY).then_inc(sem.gss, 1)
     g.scalar.wait_ge(sem.plv, 2)
-    for i, step in enumerate(STEPS):
-        for slot in step:
-            listed(g.scalar, slot)
-        for t, a, n in gathers(i, True):
-            g.scalar.activation(place(t, a, n), window(t).indirect(T.lst[:, a * L:(a + n) * L]), COPY).then_inc(sem["gs%d" % i], 1)
+    for slot in range(7):
+        listed(g.scalar, slot)
+        for t in range(VPLANES[slot], 4):
+            g.scalar.activation(place(t, slot), window(t).indirect(offsets(slot)), COPY).then_inc(sem["gs%d" % slot], 1)
 
     g.vector.wait_ge(sem.ldc, 16)
     g.vector.tensor_copy(T.cwu[:], T.cwi[:]).then_inc(sem.conv, 1)
@@ -189,51 +211,54 @@ def rank_program(g, core, T, topo):
     g.vector.wait_ge(sem.plv, 2)
     g.vector.wait_ge(sem.conv, 1)
     for t in (0, 1):
-        g.vector.tensor_copy(place(t, -1, 1), window(t).indirect(mylist)).then_inc(sem.gvs, 1)
+        g.vector.tensor_copy(place(t, -1), window(t).indirect(mylist)).then_inc(sem.gvs, 1)
     g.vector.wait_ge(sem.gvs, 2)
     g.vector.wait_ge(sem.gss, 2)
     g.vector.quantize_mx(T.wq[:, 0:S], T.wz[:, 0:S], T.w[:, 0:4 * S]).then_inc(sem.qself, 1)
 
     def quantise_x(b):
         g.vector.wait_ge(sem["ldx%d" % b], 16)
-        c = slice(b * 512, b * 512 + 512)
-        g.vector.quantize_mx(T.xq[:, c], T.xz[:, c], T.xs[:, b * 2048:b * 2048 + 2048]).then_inc(sem["xq%d" % b], 1)
+        a = half[b] * 512
+        g.vector.quantize_mx(T.xq[:, a:a + 512], T.xz[:, a:a + 512], T.xs[:, 4 * a:4 * a + 2048]).then_inc(sem["xq%d" % b], 1)
 
     quantise_x(0)
-    for i, step in enumerate(STEPS):
-        if i == len(STEPS) - 1:
+    for slot in range(7):
+        if slot == 6:
             quantise_x(1)
-        for slot in step:
-            listed(g.vector, slot)
-        for t, a, n in gathers(i, False):
-            g.vector.tensor_copy(place(t, a, n), window(t).indirect(T.lst[:, a * L:(a + n) * L])).then_inc(sem["gv%d" % i], 1)
-        g.vector.wait_ge(sem["gv%d" % i], len(gathers(i, False)))
-        g.vector.wait_ge(sem["gs%d" % i], len(gathers(i, True)))
-        a, n = step[0], len(step)
-        c = slice((a + 1) * S, (a + 1 + n) * S)
+        listed(g.vector, slot)
+        for t in range(VPLANES[slot]):
+            g.vector.tensor_copy(place(t, slot), window(t).indirect(offsets(slot))).then_inc(sem["gv%d" % slot], 1)
+        g.vector.wait_ge(sem["gv%d" % slot], VPLANES[slot])
+        g.vector.wait_ge(sem["gs%d" % slot], 4 - VPLANES[slot])
+        c = slice((slot + 1) * S, (slot + 2) * S)
         g.vector.quantize_mx(T.wq[:, c], T.wz[:, c],
-                             T.w[:, (a + 1) * 4 * S:(a + 1 + n) * 4 * S]).then_inc(sem["q%d" % i], 1)
+                             T.w[:, (slot + 1) * 4 * S:(slot + 2) * 4 * S]).then_inc(sem["q%d" % slot], 1)
 
-    def product(s, codes, scales, start, stop):
+    def product(s, codes, scales, a, start, stop):
         c = slice(s * 128, s * 128 + 128)
-        r = g.tensor.matmul_mx(T.yp[:, 0:S], T.xq[:, c], T.xz[:, c], codes, scales, start, stop)
-        if stop:
-            r.then_inc(sem.mm, 1)
+        for b in range(2):
+            m = slice(a + b * H, a + b * H + H)
+            r = g.tensor.matmul_mx(T.yp[:, b * 512:b * 512 + H], T.xq[:, c], T.xz[:, c], codes[:, m], scales[:, m], start, stop)
+            if stop:
+                r.then_inc(sem["mm%d" % b], 1)
 
     g.tensor.wait_ge(sem.xq0, 1)
-    g.tensor.wait_ge(sem.xq1, 1)
     g.tensor.wait_ge(sem.qself, 1)
-    product(rank, T.wq[:, 0:S], T.wz[:, 0:S], True, False)
+    product(rank, T.wq, T.wz, 0, True, False)
+    late = False
     for j, slot in enumerate(ARRIVAL):
         p = rank ^ ORDER[slot]
-        via = relay_of(p, slot, T, topo)
-        count = len(first_engines(p, slot, T, topo) if via is None else topo.engines(via, core))
-        g.tensor.wait_ge(sem["a%d" % slot], 2 * count)
-        c = slice(slot * S, slot * S + S)
-        product(p, T.rq[:, c], T.rz[:, c], False, j == 6)
+        if p // 4 == half[1] and not late:
+            g.tensor.wait_ge(sem.xq1, 1)
+            late = True
+        g.tensor.wait_ge(sem["a%d" % slot], sum(2 * len(hop_engines(p, slot, leg, len(way[0]), T, topo))
+                                                for leg, way in enumerate(legs_of(p, slot))))
+        product(p, T.rq, T.rz, slot * S, False, j == 6)
 
-    g.vector.wait_ge(sem.mm, 1)
-    g.vector.tensor_copy(T.ys[:], T.yp[:, 0:S]).then_inc(sem.cp, 1)
-    g.sync.wait_ge(sem.cp, 1)
+    g.vector.wait_ge(sem.mm0, 1)
+    g.vector.tensor_copy(T.ys[:, 0:H], T.yp[:, 0:H]).then_inc(sem.cp, 1)
+    g.scalar.wait_ge(sem.mm1, 1)
+    g.scalar.activation(T.ys[:, H:S], T.yp[:, 512:512 + H], COPY).then_inc(sem.cp, 1)
+    g.sync.wait_ge(sem.cp, 2)
     g.sync.dma_start(T.y[:], T.ys[:]).then_inc(sem.st, 16)
     g.sync.wait_ge(sem.st, 16)

from concourse.mybir import dt, ActivationFunctionType
from concourse.bass import DstId, RemoteDMATransfer

N = 8
S = 256
L = S // 16
H = S // 2
CORES_IN_ALL = 128
ORDER = (3, 5, 2, 7, 6, 4, 1)
DIRECT = ("qz", ((), "off"))
WAYS = ((("zq", (("near", "mate near"), "all")), ("zq", (("far", "mate far"), "all"))),
        (("zq", (("wide",), "all")), DIRECT),
        (DIRECT, ("zq", (("wide",), "rest"))),
        (("qz", (("wide",), "rest")), DIRECT),
        (DIRECT, ("qz", (("wide",), "rest"))),
        (DIRECT, DIRECT),
        (("qz", ((), "rest")),) * 2)
VPLANES = (2, 2, 1, 2, 2, 1, 1)
LISTS = ((0,), (1, 2), (3, 4), (5, 6))
ARRIVAL = (1, 2, 3, 0, 6, 4, 5)

SCRATCH = {
    "cwi": ("sbuf", [128, N * L], "int32"),
    "cwu": ("sbuf", [128, N * L], "uint16"),
    "lst": ("sbuf", [128, 7 * L], "uint16"),
    "bks": ("sbuf", [128, 512], "bfloat16"),
    "bkp": ("sbuf", [128, 512], "bfloat16"),
    "xs": ("sbuf", [128, 512 * N], "bfloat16"),
    "xq": ("sbuf", [128, 128 * N], "float8_e4m3fn_x4"),
    "xz": ("sbuf", [128, 128 * N], "uint8"),
    "w": ("sbuf", [128, 4 * S * N], "bfloat16"),
    "wq": ("sbuf", [128, S * N], "float8_e4m3fn_x4"),
    "wz": ("sbuf", [128, S * N], "uint8"),
    "rq": ("sbuf", [128, S * 7], "float8_e4m3fn_x4"),
    "rz": ("sbuf", [128, S * 7], "uint8"),
    "yp": ("psum", [128, 1024], "float32"),
    "ys": ("sbuf", [128, S], "float32"),
}
SEMAPHORES = (["ldc", "ldb", "ldx0", "ldx1", "conv", "plv", "pls", "lsent", "wsent", "fsent", "qself", "gvs", "gss",
               "xq0", "xq1", "mm0", "mm1", "cp", "st"]
              + [n % k for k in range(7) for n in ("l%d", "a%d", "gv%d", "gs%d", "q%d", "rq%d", "rz%d")])


def bits(engines):
    return sum(1 << e for e in engines)


def dest(core, topo):
    rid, pid, _ = topo.addr(core)
    return DstId(rid=rid, pnc=pid)


def parts(rank, slot):
    return WAYS[slot][rank % 2][0]


def legs_of(rank, slot):
    return WAYS[slot][rank % 2][1:]


def path(rank, slot, leg, T, topo):
    src, dst = T.cores[rank], T.cores[rank ^ ORDER[slot]]
    way = [dst]
    for kind in reversed(legs_of(rank, slot)[leg][0]):
        if kind.startswith("mate"):
            cand = [c for c in range(CORES_IN_ALL) if topo.mates(topo.chip(c), topo.chip(dst))]
        else:
            cand = topo.cores_of(src)
        cand = [c for c in cand if (topo.die(c) == topo.die(src)) == kind.endswith("near")]
        cand = [c for c in cand if T.rank_of(c) is None and topo.may_write(c, way[0])]
        reach = {c: sum(topo.may_write(c, d) for d in T.cores) for c in cand}
        cand = [c for c in cand if reach[c] == (max if kind == "wide" else min)(reach.values())]
        mine = [c for c in T.cores if topo.chip(c) == topo.chip(src)]
        way.insert(0, cand[mine.index(src) % len(cand)])
    return [src] + way


def engine_sets(rank, T, topo):
    src = T.cores[rank]
    every = max((topo.engines(src, c) for c in T.cores if c != src), key=len)
    off = min((topo.engines(src, c) for c in T.cores if c != src), key=len)
    rest = [e for e in every if e not in off]
    return {"all": every, "off": off, "rest": rest, "rest0": rest[0::2], "rest1": rest[1::2]}


def hop_engines(rank, slot, leg, hop, T, topo):
    if hop == 0:
        return engine_sets(rank, T, topo)[legs_of(rank, slot)[leg][1]]
    way = path(rank, slot, leg, T, topo)
    return topo.engines(way[hop], way[hop + 1])


def piece(codes, scales, base, rank, slot, leg, what):
    n = S // len(legs_of(rank, slot))
    c = slice(base + leg * n, base + leg * n + n)
    return codes[:, c].bitcast(dt.uint8) if what == "q" else scales[:, c]


def transfer(rank, slot, leg, hop, what, src, T, topo):
    way = path(rank, slot, leg, T, topo)
    s = T.sem["a%d" % slot] if hop + 2 == len(way) else T.sem["r%s%d" % (what, slot)]
    return RemoteDMATransfer(dst_ids=[dest(way[hop + 1], topo)], remote_sem=s, src=src,
                             dma_engine_mask=bits(hop_engines(rank, slot, leg, hop, T, topo)),
                             dst=piece(T.rq, T.rz, slot * S, rank, slot, leg, what))


def forward(g, core, T, topo):
    total = 0
    for slot in range(7):
        for rank in range(N):
            for leg in range(len(legs_of(rank, slot))):
                way = path(rank, slot, leg, T, topo)
                if core not in way:
                    continue
                hop = way.index(core)
                for what in parts(rank, slot):
                    g.wait_ge(T.sem["r%s%d" % (what, slot)], len(hop_engines(rank, slot, leg, hop - 1, T, topo)))
                    src = piece(T.rq, T.rz, slot * S, rank, slot, leg, what)
                    g.remote_dma_fused([transfer(rank, slot, leg, hop, what, src, T, topo)], local_sem=T.sem.fsent)
                    total += len(hop_engines(rank, slot, leg, hop, T, topo))
    if total:
        g.wait_ge(T.sem.fsent, total)


def list_engines(rank, T, topo):
    sets, out = engine_sets(rank, T, topo), {}
    chip = topo.chip(T.cores[rank])
    for call in LISTS:
        away = [k for k in call if topo.chip(T.cores[rank ^ ORDER[k]]) != chip]
        for k in call:
            if k in away:
                n, i = len(sets["off"]) // len(away), away.index(k)
                out[k] = sets["off"][i * n:i * n + n]
            else:
                out[k] = sets["rest"]
    return out


def rank_program(g, core, T, topo):
    rank = T.rank_of(core)
    if rank is None:
        forward(g, core, T, topo)
        return
    sem = T.sem
    COPY = ActivationFunctionType.Copy
    half = [rank // 4, 1 - rank // 4]

    def load_x(b):
        c = slice(half[b] * 2048, half[b] * 2048 + 2048)
        g.sync.dma_start(T.xs[:, c], T.x[:, c]).then_inc(sem["ldx%d" % b], 16)

    g.sync.dma_start(T.cwi[:], T.cw[:]).then_inc(sem.ldc, 16)
    g.sync.dma_start(T.bks[:], T.bk[:]).then_inc(sem.ldb, 16)
    load_x(0)

    g.wait_ge(sem.conv, 1)
    leng = list_engines(rank, T, topo)
    for call in LISTS:
        tr = []
        for slot in call:
            p = rank ^ ORDER[slot]
            tr.append(RemoteDMATransfer(dst_ids=[dest(T.cores[p], topo)], dma_engine_mask=bits(leng[slot]),
                                        remote_sem=sem["l%d" % slot], src=T.cwu[:, p * L:p * L + L],
                                        dst=T.lst[:, slot * L:slot * L + L]))
        g.remote_dma_fused(tr, local_sem=sem.lsent)
    g.sync.wait_ge(sem.lsent, sum(len(e) for e in leng.values()))
    load_x(1)

    def listed(queue, slot):
        queue.wait_ge(sem["l%d" % slot], len(list_engines(rank ^ ORDER[slot], T, topo)[slot]))

    wsent = 0
    for slot in range(7):
        g.wait_ge(sem["q%d" % slot], 1)
        legs = range(len(legs_of(rank, slot)))
        for what in parts(rank, slot):
            g.remote_dma_fused([transfer(rank, slot, leg, 0, what, piece(T.wq, T.wz, (slot + 1) * S, rank, slot, leg, what), T, topo)
                                for leg in legs], local_sem=sem.wsent)
            wsent += sum(len(hop_engines(rank, slot, leg, 0, T, topo)) for leg in legs)
    g.wait_ge(sem.wsent, wsent)

    def window(t):
        return T.bkp[:, t * 128:t * 128 + 128]

    def place(t, slot):
        a = (slot + 1) * 4 * S
        return T.w[:, a + t:a + 4 * S:4]

    def offsets(slot):
        return T.lst[:, slot * L:slot * L + L]

    g.scalar.wait_ge(sem.ldb, 16)
    for t in (2, 3):
        g.scalar.activation(T.bkp[:, t * 128:t * 128 + 128], T.bks[:, t:512:4], COPY).then_inc(sem.pls, 1)
    mylist = T.cwu[:, rank * L:rank * L + L]
    g.scalar.wait_ge(sem.pls, 2)
    g.scalar.wait_ge(sem.conv, 1)
    for t in (2, 3):
        g.scalar.activation(place(t, -1), window(t).indirect(mylist), COPY).then_inc(sem.gss, 1)
    g.scalar.wait_ge(sem.plv, 2)
    for slot in range(7):
        listed(g.scalar, slot)
        for t in range(VPLANES[slot], 4):
            g.scalar.activation(place(t, slot), window(t).indirect(offsets(slot)), COPY).then_inc(sem["gs%d" % slot], 1)

    g.vector.wait_ge(sem.ldc, 16)
    g.vector.tensor_copy(T.cwu[:], T.cwi[:]).then_inc(sem.conv, 1)
    g.vector.wait_ge(sem.ldb, 16)
    for t in (0, 1):
        g.vector.tensor_copy(T.bkp[:, t * 128:t * 128 + 128], T.bks[:, t:512:4]).then_inc(sem.plv, 1)
    g.vector.wait_ge(sem.plv, 2)
    g.vector.wait_ge(sem.conv, 1)
    for t in (0, 1):
        g.vector.tensor_copy(place(t, -1), window(t).indirect(mylist)).then_inc(sem.gvs, 1)
    g.vector.wait_ge(sem.gvs, 2)
    g.vector.wait_ge(sem.gss, 2)
    g.vector.quantize_mx(T.wq[:, 0:S], T.wz[:, 0:S], T.w[:, 0:4 * S]).then_inc(sem.qself, 1)

    def quantise_x(b):
        g.vector.wait_ge(sem["ldx%d" % b], 16)
        a = half[b] * 512
        g.vector.quantize_mx(T.xq[:, a:a + 512], T.xz[:, a:a + 512], T.xs[:, 4 * a:4 * a + 2048]).then_inc(sem["xq%d" % b], 1)

    quantise_x(0)
    for slot in range(7):
        if slot == 6:
            quantise_x(1)
        listed(g.vector, slot)
        for t in range(VPLANES[slot]):
            g.vector.tensor_copy(place(t, slot), window(t).indirect(offsets(slot))).then_inc(sem["gv%d" % slot], 1)
        g.vector.wait_ge(sem["gv%d" % slot], VPLANES[slot])
        g.vector.wait_ge(sem["gs%d" % slot], 4 - VPLANES[slot])
        c = slice((slot + 1) * S, (slot + 2) * S)
        g.vector.quantize_mx(T.wq[:, c], T.wz[:, c],
                             T.w[:, (slot + 1) * 4 * S:(slot + 2) * 4 * S]).then_inc(sem["q%d" % slot], 1)

    def product(s, codes, scales, a, start, stop):
        c = slice(s * 128, s * 128 + 128)
        for b in range(2):
            m = slice(a + b * H, a + b * H + H)
            r = g.tensor.matmul_mx(T.yp[:, b * 512:b * 512 + H], T.xq[:, c], T.xz[:, c], codes[:, m], scales[:, m], start, stop)
            if stop:
                r.then_inc(sem["mm%d" % b], 1)

    g.tensor.wait_ge(sem.xq0, 1)
    g.tensor.wait_ge(sem.qself, 1)
    product(rank, T.wq, T.wz, 0, True, False)
    late = False
    for j, slot in enumerate(ARRIVAL):
        p = rank ^ ORDER[slot]
        if p // 4 == half[1] and not late:
            g.tensor.wait_ge(sem.xq1, 1)
            late = True
        g.tensor.wait_ge(sem["a%d" % slot], sum(2 * len(hop_engines(p, slot, leg, len(way[0]), T, topo))
                                                for leg, way in enumerate(legs_of(p, slot))))
        product(p, T.rq, T.rz, slot * S, False, j == 6)

    g.vector.wait_ge(sem.mm0, 1)
    g.vector.tensor_copy(T.ys[:, 0:H], T.yp[:, 0:H]).then_inc(sem.cp, 1)
    g.scalar.wait_ge(sem.mm1, 1)
    g.scalar.activation(T.ys[:, H:S], T.yp[:, 512:512 + H], COPY).then_inc(sem.cp, 1)
    g.sync.wait_ge(sem.cp, 2)
    g.sync.dma_start(T.y[:], T.ys[:]).then_inc(sem.st, 16)
    g.sync.wait_ge(sem.st, 16)
